import numpy as np, ml_dtypes
CORES = [1,17,65,89,97,113]
N = 6
import mx_ref
NC = 256
BF = ml_dtypes.bfloat16
def setup_inputs(rng):
    def f(*shape):
        return mx_ref.flush((rng.standard_normal(shape, dtype=np.float32) * np.exp2(rng.integers(-2, 3, shape[:-1] + (1,)))).astype(BF))
    return {"u": f(N, 128, 512), "v": f(N, 128, 512), "x": f(N, 128, 4 * NC)}
def setup_inputs_blocks(rng):
    d = setup_inputs(rng)
    for k in ("u", "v", "x"): d[k] = mx_ref.spread(d[k], rng, 4)
    return d
def setup_inputs_wide(rng):
    d = setup_inputs(rng)
    for k in ("u", "v", "x"): d[k] = mx_ref.flush((d[k].astype(np.float32) * np.exp2(rng.integers(-8, 9, (N, 1, 1))).astype(np.float32)).astype(BF))
    return d
def setup_inputs_zeros(rng):
    d = setup_inputs(rng); v = d["x"].reshape(N, 128, -1, 4).copy()
    v[np.broadcast_to((rng.random((N, 1, v.shape[2], 1)) < 0.33), v.shape)] = 0
    d["x"] = v.reshape(d["x"].shape)
    return d
def reference(u, v, x):
    QX = [mx_ref.quantize(x[j]) for j in range(N)]
    y = np.zeros((N, 128, N * NC), np.float32)
    for r in range(N):
        qu, qv = mx_ref.quantize(u[r]), mx_ref.quantize(v[r])
        for j in range(N):
            y[r][:, NC * j:NC * j + NC] = np.maximum(mx_ref.matmul(qu, QX[j]), np.float32(0)) * mx_ref.matmul(qv, QX[j])
    return {"y": y}

@@ -1,0 +1,163 @@
+from concourse.bass import DstId, RemoteDMATransfer
+from concourse.mybir import dt, AluOpType, ActivationFunctionType
+
+N = 6
+NC = 256
+BANK = 512
+NB = 4
+
+SCRATCH = {
+    "xb": ("sbuf", [128, 4 * NC], "bfloat16"),
+    "ub": ("sbuf", [128, 512], "bfloat16"),
+    "vb": ("sbuf", [128, 512], "bfloat16"),
+    "xq": ("sbuf", [128, N * NC], "float8_e4m3fn_x4"),
+    "xs": ("sbuf", [128, N * NC], "uint8"),
+    "uq": ("sbuf", [128, 128], "float8_e4m3fn_x4"),
+    "us": ("sbuf", [128, 128], "uint8"),
+    "vq": ("sbuf", [128, 128], "float8_e4m3fn_x4"),
+    "vs": ("sbuf", [128, 128], "uint8"),
+    "pu": ("psum", [128, NB * BANK], "float32"),
+    "pv": ("psum", [128, NB * BANK], "float32"),
+    "ru": ("sbuf", [128, N * NC], "float32"),
+    "yb": ("sbuf", [128, N * NC], "float32"),
+}
+SEMAPHORES = (["lx", "lu", "lv", "qx", "qw", "sent", "st"]
+              + ["%s%d" % (p, k) for p in ("c", "s", "mu", "mv", "rd", "md") for k in range(N)])
+
+
+def _bits(mask):
+    return [1 << b for b in range(mask.bit_length()) if (mask >> b) & 1]
+
+
+def _common(topo, src, dsts):
+    m = topo.mask(src, dsts[0])
+    for d in dsts[1:]:
+        m &= topo.mask(src, d)
+    return m
+
+
+def _plan(cores, topo):
+    n = len(cores)
+    calls, arrive, port = {}, {}, {}
+    for r, src in enumerate(cores):
+        others = [(r + k) % n for k in range(1, n)]
+        direct = [cores[d] for d in others if topo.may_write(src, cores[d])]
+        far = [cores[d] for d in others if not topo.may_write(src, cores[d])]
+        near = [c for c in range(topo.CHIPS * topo.CORES_PER_CHIP)
+                if topo.chip(c) == topo.chip(src) and c not in cores
+                and all(topo.may_write(c, d) for d in far)]
+        same = [c for c in near if topo.die(c) == topo.die(src)]
+        cross = [c for c in near if topo.die(c) != topo.die(src)]
+        job = {}
+        if len(far) == 1:
+            key = topo.chip(far[0])
+            load = port.setdefault(key, {topo.die(same[0]): 0, topo.die(cross[0]): 0})
+            h = same[0] if load[topo.die(same[0])] <= load[topo.die(cross[0])] else cross[0]
+            load[topo.die(h)] += 1
+            job[h] = {"s": far, "c": far}
+            order = {"s": [h], "c": [h]}
+        elif far:
+            a, b, c, d = same[0], cross[0], same[1], cross[1]
+            q = (len(far) - 1) // 2
+            job[a] = {"s": [], "c": far[:q]}
+            job[b] = {"s": [], "c": far[q:2 * q]}
+            job[c] = {"s": far[2 * q - 1:], "c": far[2 * q:]}
+            job[d] = {"s": far[:2 * q - 1], "c": []}
+            order = {"s": [d, c], "c": [a, b, c]}
+        else:
+            order = {"s": [], "c": []}
+        mine = calls.setdefault(src, [])
+        for kind in ("s", "c"):
+            tr = []
+            off = _common(topo, src, direct) if direct else 0
+            if order[kind]:
+                tr.append((_common(topo, src, order[kind]) & ~off, order[kind]))
+            if direct:
+                tr.append((off, direct))
+            mine.append((r, kind, tr))
+        for h in job:
+            for kind in ("s", "c"):
+                if job[h][kind]:
+                    calls.setdefault(h, []).append((r, kind, [(_common(topo, h, job[h][kind]), job[h][kind])]))
+    for c in calls:
+        for r, kind, tr in calls[c]:
+            for mask, dsts in tr:
+                for d in dsts:
+                    arrive[(d, r, kind)] = arrive.get((d, r, kind), 0) + len(_bits(mask))
+    return calls, arrive
+
+
+def rank_program(g, core, T, topo):
+    cores = list(T.cores)
+    calls, arrive = _plan(cores, topo)
+    if core not in calls:
+        return
+    rank = T.rank_of(core)
+    sem = T.sem
+
+    def codes(j):
+        return T.xq[:, j * NC:(j + 1) * NC]
+
+    def plane(j):
+        return T.xs[:, j * NC:(j + 1) * NC]
+
+    def piece(kind, j):
+        return plane(j) if kind == "s" else codes(j).bitcast(dt.uint8)
+
+    left = 0
+    if rank is not None:
+        g.wait_ge(sem.qx, 1)
+    for r, kind, tr in calls[core]:
+        if cores[r] != core:
+            g.wait_ge(sem["%s%d" % (kind, r)], arrive[(core, r, kind)])
+        ts = []
+        for mask, dsts in tr:
+            ids = []
+            for d in dsts:
+                rid, pid, _se = topo.addr(d)
+                ids.append(DstId(rid=rid, pnc=pid))
+            ts.append(RemoteDMATransfer(dst_ids=ids, dma_engine_mask=mask, remote_sem=sem["%s%d" % (kind, r)],
+                                        srcs=[piece(kind, r)], dsts=[piece(kind, r) for _d in dsts]))
+            left += len(_bits(mask))
+        g.remote_dma_fused(ts, local_sem=sem.sent)
+    g.wait_ge(sem.sent, left)
+    if rank is None:
+        return
+
+    g.sync.dma_start(T.xb[:], T.x[:]).then_inc(sem.lx, 16)
+    g.sync.dma_start(T.ub[:], T.u[:]).then_inc(sem.lu, 16)
+    g.sync.dma_start(T.vb[:], T.v[:]).then_inc(sem.lv, 16)
+
+    g.vector.wait_ge(sem.lx, 16)
+    g.vector.quantize_mx(codes(rank), plane(rank), T.xb[:]).then_inc(sem.qx, 1)
+    g.vector.wait_ge(sem.lu, 16)
+    g.vector.quantize_mx(T.uq[:], T.us[:], T.ub[:]).then_inc(sem.qw, 1)
+    g.vector.wait_ge(sem.lv, 16)
+    g.vector.quantize_mx(T.vq[:], T.vs[:], T.vb[:]).then_inc(sem.qw, 1)
+
+    back = [(rank - k) % N for k in range(1, N)]
+    seq = ([rank] + [j for j in back if topo.may_write(cores[j], core)]
+           + [j for j in back if not topo.may_write(cores[j], core)])
+
+    g.tensor.wait_ge(sem.qx, 1)
+    g.tensor.wait_ge(sem.qw, 2)
+    for k, j in enumerate(seq):
+        b = (k % NB) * BANK
+        pu, pv = T.pu[:, b:b + NC], T.pv[:, b:b + NC]
+        ru, yb = T.ru[:, j * NC:(j + 1) * NC], T.yb[:, j * NC:(j + 1) * NC]
+        if j != rank:
+            g.tensor.wait_ge(sem["s%d" % j], arrive[(core, j, "s")])
+            g.tensor.wait_ge(sem["c%d" % j], arrive[(core, j, "c")])
+        if k >= NB:
+            g.tensor.wait_ge(sem["rd%d" % (k - NB)], 1)
+            g.tensor.wait_ge(sem["md%d" % (k - NB)], 1)
+        g.tensor.matmul_mx(pu, T.uq[:], T.us[:], codes(j), plane(j), True, True).then_inc(sem["mu%d" % k], 1)
+        g.tensor.matmul_mx(pv, T.vq[:], T.vs[:], codes(j), plane(j), True, True).then_inc(sem["mv%d" % k], 1)
+        g.scalar.wait_ge(sem["mu%d" % k], 1)
+        g.scalar.activation(ru, pu, ActivationFunctionType.Relu).then_inc(sem["rd%d" % k], 1)
+        g.vector.wait_ge(sem["mv%d" % k], 1)
+        g.vector.wait_ge(sem["rd%d" % k], 1)
+        g.vector.tensor_tensor(yb, ru, pv, AluOpType.mult).then_inc(sem["md%d" % k], 1)
+        g.sync.wait_ge(sem["md%d" % k], 1)
+        g.sync.dma_start(T.y[:, j * NC:(j + 1) * NC], yb).then_inc(sem.st, 16)
+    g.sync.wait_ge(sem.st, 16 * N)

@@ -5,6 +5,7 @@ N = 6
 NC = 256
 BANK = 512
 NB = 4
+SHED = 1
 
 SCRATCH = {
     "xb": ("sbuf", [128, 4 * NC], "bfloat16"),
@@ -38,58 +39,69 @@ def _common(topo, src, dsts):
 
 def _plan(cores, topo):
     n = len(cores)
-    calls, arrive, port = {}, {}, {}
+    calls, arrive, when, port, lane = {}, {}, {}, {}, {}
     for r, src in enumerate(cores):
-        others = [(r + k) % n for k in range(1, n)]
-        direct = [cores[d] for d in others if topo.may_write(src, cores[d])]
-        far = [cores[d] for d in others if not topo.may_write(src, cores[d])]
-        near = [c for c in range(topo.CHIPS * topo.CORES_PER_CHIP)
-                if topo.chip(c) == topo.chip(src) and c not in cores
-                and all(topo.may_write(c, d) for d in far)]
+        others = [cores[(r + k) % n] for k in range(1, n)]
+        direct = [d for d in others if topo.may_write(src, d)]
+        far = [d for d in others if not topo.may_write(src, d)]
+        chipmates = [c for c in range(topo.CHIPS * topo.CORES_PER_CHIP)
+                     if topo.chip(c) == topo.chip(src) and c not in cores]
+        near = [c for c in chipmates if all(topo.may_write(c, d) for d in far)]
         same = [c for c in near if topo.die(c) == topo.die(src)]
         cross = [c for c in near if topo.die(c) != topo.die(src)]
         job = {}
+        served = []
         if len(far) == 1:
-            key = topo.chip(far[0])
-            load = port.setdefault(key, {topo.die(same[0]): 0, topo.die(cross[0]): 0})
+            load = port.setdefault(topo.chip(far[0]), {topo.die(same[0]): 0, topo.die(cross[0]): 0})
             h = same[0] if load[topo.die(same[0])] <= load[topo.die(cross[0])] else cross[0]
             load[topo.die(h)] += 1
+            lane[(far[0], r)] = topo.die(h)
             job[h] = {"s": far, "c": far}
-            order = {"s": [h], "c": [h]}
+            served = [h]
         elif far:
-            a, b, c, d = same[0], cross[0], same[1], cross[1]
-            q = (len(far) - 1) // 2
-            job[a] = {"s": [], "c": far[:q]}
-            job[b] = {"s": [], "c": far[q:2 * q]}
-            job[c] = {"s": far[2 * q - 1:], "c": far[2 * q:]}
-            job[d] = {"s": far[:2 * q - 1], "c": []}
-            order = {"s": [d, c], "c": [a, b, c]}
-        else:
-            order = {"s": [], "c": []}
+            served = [c for pair in zip(same, cross) for c in pair]
+            for h in served:
+                job[h] = {"s": [], "c": []}
+            for i, d in enumerate(far):
+                if i < len(served):
+                    job[served[i]]["s"].append(d)
+                    job[served[i]]["c"].append(d)
+                else:
+                    job[served[(2 * i) % len(served)]]["c"].append(d)
+                    job[served[(2 * i + 1) % len(served)]]["s"].append(d)
+        shed = []
+        if len(direct) > SHED > 0:
+            direct, shed = direct[:-SHED], direct[-SHED:]
+            h2 = [c for c in chipmates if topo.die(c) != topo.die(src) and c not in job
+                  and all(topo.may_write(c, d) for d in shed)][-1]
+            job[h2] = {"s": shed, "c": shed}
+            served = served + [h2]
+        for k, d in enumerate(others):
+            when[(d, r)] = (0 if d in direct else 1 if d in shed else 2, 0, k)
+        off = _common(topo, src, direct) if direct else 0
+        inner = [(_common(topo, src, served) & ~off, served)] if served else []
+        outer = [(off, direct)] if direct else []
         mine = calls.setdefault(src, [])
-        for kind in ("s", "c"):
-            tr = []
-            off = _common(topo, src, direct) if direct else 0
-            if order[kind]:
-                tr.append((_common(topo, src, order[kind]) & ~off, order[kind]))
-            if direct:
-                tr.append((off, direct))
-            mine.append((r, kind, tr))
-        for h in job:
+        for tr in (inner, outer):
+            if tr:
+                mine.append((r, "s", tr))
+        mine.append((r, "c", inner + outer))
+        for h in served:
             for kind in ("s", "c"):
-                if job[h][kind]:
-                    calls.setdefault(h, []).append((r, kind, [(_common(topo, h, job[h][kind]), job[h][kind])]))
+                calls.setdefault(h, []).append((r, kind, [(_common(topo, h, job[h][kind]), job[h][kind])]))
+    for d, r in lane:
+        when[(d, r)] = (2, port[topo.chip(d)][lane[(d, r)]], when[(d, r)][2])
     for c in calls:
         for r, kind, tr in calls[c]:
             for mask, dsts in tr:
                 for d in dsts:
                     arrive[(d, r, kind)] = arrive.get((d, r, kind), 0) + len(_bits(mask))
-    return calls, arrive
+    return calls, arrive, when
 
 
 def rank_program(g, core, T, topo):
     cores = list(T.cores)
-    calls, arrive = _plan(cores, topo)
+    calls, arrive, when = _plan(cores, topo)
     if core not in calls:
         return
     rank = T.rank_of(core)
@@ -135,9 +147,7 @@ def rank_program(g, core, T, topo):
     g.vector.wait_ge(sem.lv, 16)
     g.vector.quantize_mx(T.vq[:], T.vs[:], T.vb[:]).then_inc(sem.qw, 1)
 
-    back = [(rank - k) % N for k in range(1, N)]
-    seq = ([rank] + [j for j in back if topo.may_write(cores[j], core)]
-           + [j for j in back if not topo.may_write(cores[j], core)])
+    seq = [rank] + sorted([j for j in range(N) if j != rank], key=lambda j: when[(core, j)])
 
     g.tensor.wait_ge(sem.qx, 1)
     g.tensor.wait_ge(sem.qw, 2)

from concourse.bass import DstId, RemoteDMATransfer
from concourse.mybir import dt, AluOpType, ActivationFunctionType

N = 6
NC = 256
BANK = 512
NB = 4
SHED = 1

SCRATCH = {
    "xb": ("sbuf", [128, 4 * NC], "bfloat16"),
    "ub": ("sbuf", [128, 512], "bfloat16"),
    "vb": ("sbuf", [128, 512], "bfloat16"),
    "xq": ("sbuf", [128, N * NC], "float8_e4m3fn_x4"),
    "xs": ("sbuf", [128, N * NC], "uint8"),
    "uq": ("sbuf", [128, 128], "float8_e4m3fn_x4"),
    "us": ("sbuf", [128, 128], "uint8"),
    "vq": ("sbuf", [128, 128], "float8_e4m3fn_x4"),
    "vs": ("sbuf", [128, 128], "uint8"),
    "pu": ("psum", [128, NB * BANK], "float32"),
    "pv": ("psum", [128, NB * BANK], "float32"),
    "ru": ("sbuf", [128, N * NC], "float32"),
    "yb": ("sbuf", [128, N * NC], "float32"),
}
SEMAPHORES = (["lx", "lu", "lv", "qx", "qw", "sent", "st"]
              + ["%s%d" % (p, k) for p in ("c", "s", "mu", "mv", "rd", "md") for k in range(N)])


def _bits(mask):
    return [1 << b for b in range(mask.bit_length()) if (mask >> b) & 1]


def _common(topo, src, dsts):
    m = topo.mask(src, dsts[0])
    for d in dsts[1:]:
        m &= topo.mask(src, d)
    return m


def _plan(cores, topo):
    n = len(cores)
    calls, arrive, when, port, lane = {}, {}, {}, {}, {}
    for r, src in enumerate(cores):
        others = [cores[(r + k) % n] for k in range(1, n)]
        direct = [d for d in others if topo.may_write(src, d)]
        far = [d for d in others if not topo.may_write(src, d)]
        chipmates = [c for c in range(topo.CHIPS * topo.CORES_PER_CHIP)
                     if topo.chip(c) == topo.chip(src) and c not in cores]
        near = [c for c in chipmates if all(topo.may_write(c, d) for d in far)]
        same = [c for c in near if topo.die(c) == topo.die(src)]
        cross = [c for c in near if topo.die(c) != topo.die(src)]
        job = {}
        served = []
        if len(far) == 1:
            load = port.setdefault(topo.chip(far[0]), {topo.die(same[0]): 0, topo.die(cross[0]): 0})
            h = same[0] if load[topo.die(same[0])] <= load[topo.die(cross[0])] else cross[0]
            load[topo.die(h)] += 1
            lane[(far[0], r)] = topo.die(h)
            job[h] = {"s": far, "c": far}
            served = [h]
        elif far:
            served = [c for pair in zip(same, cross) for c in pair]
            for h in served:
                job[h] = {"s": [], "c": []}
            for i, d in enumerate(far):
                if i < len(served):
                    job[served[i]]["s"].append(d)
                    job[served[i]]["c"].append(d)
                else:
                    job[served[(2 * i) % len(served)]]["c"].append(d)
                    job[served[(2 * i + 1) % len(served)]]["s"].append(d)
        shed = []
        if len(direct) > SHED > 0:
            direct, shed = direct[:-SHED], direct[-SHED:]
            h2 = [c for c in chipmates if topo.die(c) != topo.die(src) and c not in job
                  and all(topo.may_write(c, d) for d in shed)][-1]
            job[h2] = {"s": shed, "c": shed}
            served = served + [h2]
        for k, d in enumerate(others):
            when[(d, r)] = (0 if d in direct else 1 if d in shed else 2, 0, k)
        off = _common(topo, src, direct) if direct else 0
        inner = [(_common(topo, src, served) & ~off, served)] if served else []
        outer = [(off, direct)] if direct else []
        mine = calls.setdefault(src, [])
        for tr in (inner, outer):
            if tr:
                mine.append((r, "s", tr))
        mine.append((r, "c", inner + outer))
        for h in served:
            for kind in ("s", "c"):
                calls.setdefault(h, []).append((r, kind, [(_common(topo, h, job[h][kind]), job[h][kind])]))
    for d, r in lane:
        when[(d, r)] = (2, port[topo.chip(d)][lane[(d, r)]], when[(d, r)][2])
    for c in calls:
        for r, kind, tr in calls[c]:
            for mask, dsts in tr:
                for d in dsts:
                    arrive[(d, r, kind)] = arrive.get((d, r, kind), 0) + len(_bits(mask))
    return calls, arrive, when


def rank_program(g, core, T, topo):
    cores = list(T.cores)
    calls, arrive, when = _plan(cores, topo)
    if core not in calls:
        return
    rank = T.rank_of(core)
    sem = T.sem

    def codes(j):
        return T.xq[:, j * NC:(j + 1) * NC]

    def plane(j):
        return T.xs[:, j * NC:(j + 1) * NC]

    def piece(kind, j):
        return plane(j) if kind == "s" else codes(j).bitcast(dt.uint8)

    left = 0
    if rank is not None:
        g.wait_ge(sem.qx, 1)
    for r, kind, tr in calls[core]:
        if cores[r] != core:
            g.wait_ge(sem["%s%d" % (kind, r)], arrive[(core, r, kind)])
        ts = []
        for mask, dsts in tr:
            ids = []
            for d in dsts:
                rid, pid, _se = topo.addr(d)
                ids.append(DstId(rid=rid, pnc=pid))
            ts.append(RemoteDMATransfer(dst_ids=ids, dma_engine_mask=mask, remote_sem=sem["%s%d" % (kind, r)],
                                        srcs=[piece(kind, r)], dsts=[piece(kind, r) for _d in dsts]))
            left += len(_bits(mask))
        g.remote_dma_fused(ts, local_sem=sem.sent)
    g.wait_ge(sem.sent, left)
    if rank is None:
        return

    g.sync.dma_start(T.xb[:], T.x[:]).then_inc(sem.lx, 16)
    g.sync.dma_start(T.ub[:], T.u[:]).then_inc(sem.lu, 16)
    g.sync.dma_start(T.vb[:], T.v[:]).then_inc(sem.lv, 16)

    g.vector.wait_ge(sem.lx, 16)
    g.vector.quantize_mx(codes(rank), plane(rank), T.xb[:]).then_inc(sem.qx, 1)
    g.vector.wait_ge(sem.lu, 16)
    g.vector.quantize_mx(T.uq[:], T.us[:], T.ub[:]).then_inc(sem.qw, 1)
    g.vector.wait_ge(sem.lv, 16)
    g.vector.quantize_mx(T.vq[:], T.vs[:], T.vb[:]).then_inc(sem.qw, 1)

    seq = [rank] + sorted([j for j in range(N) if j != rank], key=lambda j: when[(core, j)])

    g.tensor.wait_ge(sem.qx, 1)
    g.tensor.wait_ge(sem.qw, 2)
    for k, j in enumerate(seq):
        b = (k % NB) * BANK
        pu, pv = T.pu[:, b:b + NC], T.pv[:, b:b + NC]
        ru, yb = T.ru[:, j * NC:(j + 1) * NC], T.yb[:, j * NC:(j + 1) * NC]
        if j != rank:
            g.tensor.wait_ge(sem["s%d" % j], arrive[(core, j, "s")])
            g.tensor.wait_ge(sem["c%d" % j], arrive[(core, j, "c")])
        if k >= NB:
            g.tensor.wait_ge(sem["rd%d" % (k - NB)], 1)
            g.tensor.wait_ge(sem["md%d" % (k - NB)], 1)
        g.tensor.matmul_mx(pu, T.uq[:], T.us[:], codes(j), plane(j), True, True).then_inc(sem["mu%d" % k], 1)
        g.tensor.matmul_mx(pv, T.vq[:], T.vs[:], codes(j), plane(j), True, True).then_inc(sem["mv%d" % k], 1)
        g.scalar.wait_ge(sem["mu%d" % k], 1)
        g.scalar.activation(ru, pu, ActivationFunctionType.Relu).then_inc(sem["rd%d" % k], 1)
        g.vector.wait_ge(sem["mv%d" % k], 1)
        g.vector.wait_ge(sem["rd%d" % k], 1)
        g.vector.tensor_tensor(yb, ru, pv, AluOpType.mult).then_inc(sem["md%d" % k], 1)
        g.sync.wait_ge(sem["md%d" % k], 1)
        g.sync.dma_start(T.y[:, j * NC:(j + 1) * NC], yb).then_inc(sem.st, 16)
    g.sync.wait_ge(sem.st, 16 * N)
